import numpy as np
import ml_dtypes


def mxq(x, axis, fmt="e4m3"):
    dtype, down = {"e4m3": (ml_dtypes.float8_e4m3fn, 7), "e5m2": (ml_dtypes.float8_e5m2, 14)}[fmt]
    v = np.moveaxis(np.asarray(x, np.float32).astype(ml_dtypes.bfloat16).astype(np.float64), axis, -1)
    blocks = v.reshape(v.shape[:-1] + (-1, 32))
    amax = np.abs(blocks).max(-1, keepdims=True)
    byte = np.maximum(np.where(amax > 0, np.frexp(amax)[1] - 1 + 127, 0) - down, 1)
    scale = np.exp2(byte - 127.0)
    codes = (blocks / scale).astype(np.float32).astype(dtype).astype(np.float64)
    return np.moveaxis((codes * scale).reshape(v.shape), -1, axis)


WIDE = False


def mx_kscale(k):
    if not WIDE:
        return np.ones(k)
    levels = np.array([10, -10, 5, -5, 0])
    if k % 512:
        return np.exp2(np.random.permutation(np.resize(levels, k // 32))).repeat(32)
    a = np.empty((k // 512, 16))
    for p in range(k // 512):
        a[p, :8] = np.random.permutation(np.resize(levels, 8))
        for g in range(8):
            far = levels[np.abs(levels - a[p, g]) >= 10]
            a[p, g + 8] = far[np.random.randint(len(far))]
    return np.exp2(a.ravel()).repeat(32)


BF16 = ml_dtypes.bfloat16


def bf(x):
    return np.asarray(x, np.float32).astype(BF16)


def f64(x):
    return np.asarray(x).astype(np.float64)


E2M1 = np.array([0.0, 0.5, 1.0, 1.5, 2.0, 3.0, 4.0, 6.0, -0.0, -0.5, -1.0, -1.5, -2.0, -3.0, -4.0, -6.0])


def pack_weight(w, fmt):
    k, n = w.shape
    w = f64(bf(w)).reshape(k // 32, 32, n)
    amax = np.abs(w).max(1)
    if fmt == "e4m3":
        byte = np.frexp(amax)[1] - 1 + 127 - 7
    else:
        mant, ex = np.frexp(amax / 6.0)
        byte = np.where(mant > 0.5, ex, ex - 1) + 127
    byte = np.clip(np.where(amax > 0, byte, 1), 1, 254)
    scaled = (w * np.exp2(127.0 - byte)[:, None, :]).reshape(k, n).astype(np.float32)
    by_word = np.ascontiguousarray(scaled.reshape(k // 512, 128, 4, n).transpose(0, 1, 3, 2))
    if fmt == "e4m3":
        words = by_word.astype(ml_dtypes.float8_e4m3fn).view(np.uint8)
    else:
        c = by_word.astype(ml_dtypes.float4_e2m1fn).view(np.uint8) & 0xF
        words = c[..., 0::2] | (c[..., 1::2] << 4)
    return np.ascontiguousarray(words), np.ascontiguousarray(byte.astype(np.uint8).reshape(k // 512, 16, n))


def unpack_weight(words, scales, fmt):
    g, p, n, _ = words.shape
    if fmt == "e4m3":
        vals = np.ascontiguousarray(words).view(ml_dtypes.float8_e4m3fn).astype(np.float64)
    else:
        nib = np.empty((g, p, n, 4), np.uint8)
        nib[..., 0::2] = words & 0xF
        nib[..., 1::2] = words >> 4
        vals = E2M1[nib]
    vals = vals * np.repeat(np.exp2(scales.astype(np.float64) - 127.0), 8, axis=1)[..., None]
    return vals.transpose(0, 1, 3, 2).reshape(g * 512, n)
def pack4(w):
    words, scales = pack_weight(w, "e2m1")
    return words.reshape(words.shape[0], 128, -1), scales


def unpack4(words, scales):
    return unpack_weight(words.reshape(words.shape[0], 128, -1, 2), scales, "e2m1")


P, Q = 1536, 512


def setup_inputs():
    s, t = mx_kscale(P), mx_kscale(Q)
    c = np.random.standard_normal((P, Q)) * s[:, None] * t
    f = 0.35 * np.random.standard_normal((P, P)) / np.sqrt(P) / s[:, None] * s
    d = 0.5 * np.random.standard_normal((Q, Q)) / np.sqrt(Q) / t[:, None] * t
    b = 0.35 * np.random.standard_normal((P, P)) / np.sqrt(P) / s[:, None] * s
    f_words, f_scales = pack4(f)
    d_words, d_scales = pack4(d)
    b_words, b_scales = pack4(b)
    return {"c": bf(c),
            "f_words": f_words, "f_scales": f_scales,
            "d_words": d_words, "d_scales": d_scales,
            "b_words": b_words, "b_scales": b_scales,
            "v": bf((1 + 0.1 * np.random.standard_normal(P)) / s),
            "r": bf((1 + 0.1 * np.random.standard_normal(Q)) / t)}


def reference(c, f_words, f_scales, d_words, d_scales, b_words, b_scales, v, r):
    F = unpack4(f_words, f_scales)
    D = unpack4(d_words, d_scales)
    B = unpack4(b_words, b_scales)
    c0 = f64(c)
    c1 = c0 + (F.T @ mxq(c0, 0, "e4m3"))
    push = mxq(c1, 1, "e4m3") @ D
    c2 = c1 - np.maximum(push, 0.0)
    c3 = c2 + (B.T @ mxq(c2, 0, "e4m3"))
    return c3 * f64(v)[:, None] * f64(r)[None, :]

from contextlib import ExitStack

import concourse.mybir as mybir
from concourse.masks import make_identity

P, Q = 1536, 512
FLOPS = 2 * (2 * P * P * Q + P * Q * Q)

F32 = mybir.dt.float32
BF16 = mybir.dt.bfloat16
I32 = mybir.dt.int32
U32 = mybir.dt.uint32
U8 = mybir.dt.uint8
FP8X4 = mybir.dt.float8_e4m3fn_x4
FP4X4 = mybir.dt.float4_e2m1fn_x4
ALU = mybir.AluOpType
COPY = mybir.ActivationFunctionType.Copy

PART = 128
G = 3
NT = 4
JB = 512
IL_SPLIT = 80
RELAY_A = []
RELAY_X = []
I_ENGINE = ["gsss", "sggs", "ggsv"]
R_ENGINE = ["ggg", "ggg", "gsg", "sgv"]
O_SCALAR = [0, 2, 4, 5, 6, 7, 11]
ORDER = [
    ("CT", 0),
    ("IL", 0, 0),
    ("CT", 1),
    ("IL", 0, 1),
    ("QC", 0),
    ("S1", 0, 0, 0),
    ("IL", 1, 1),
    ("S1", 0, 0, 3),
    ("IL", 1, 0),
    ("D", 0),
    ("S1", 0, 0, 1),
    ("KC", 1, 0),
    ("KC", 0, 1),
    ("S1", 0, 0, 2),
    ("QC", 1),
    ("CT", 2),
    ("IL", 2, 0),
    ("S1", 1, 0, 0),
    ("S1", 1, 0, 1),
    ("S1", 1, 0, 3),
    ("IL", 2, 1),
    ("KC", 0, 0),
    ("S1", 0, 1, 0),
    ("D", 3),
    ("QC", 2),
    ("D", 2),
    ("S1", 2, 0, 1),
    ("S1", 1, 0, 2),
    ("S1", 2, 0, 3),
    ("S1", 2, 0, 2),
    ("D", 1),
    ("A", 0, 1),
    ("S1", 1, 1, 0),
    ("S1", 2, 1, 0),
    ("KC", 1, 1),
    ("S1", 2, 0, 0),
    ("A", 0, 3),
    ("S1", 0, 1, 2),
    ("KC", 2, 0),
    ("S1", 0, 2, 0),
    ("A", 0, 2),
    ("A", 0, 0),
    ("A", 1, 0),
    ("KC", 2, 1),
    ("S1", 1, 1, 2),
    ("S1", 2, 1, 2),
    ("S1", 0, 1, 1),
    ("S1", 1, 2, 0),
    ("S1", 2, 2, 0),
    ("I", 0, 1),
    ("A", 1, 2),
    ("S1", 1, 1, 1),
    ("S1", 2, 1, 1),
    ("I", 0, 0),
    ("S1", 0, 1, 3),
    ("S1", 1, 1, 3),
    ("Q1", 0, 0),
    ("I", 0, 3),
    ("A", 2, 0),
    ("S1", 2, 1, 3),
    ("S1", 0, 2, 3),
    ("A", 1, 1),
    ("I", 0, 2),
    ("S1", 1, 2, 3),
    ("A", 1, 3),
    ("S1", 2, 2, 3),
    ("Q1", 0, 1),
    ("I", 1, 1),
    ("S1", 0, 2, 1),
    ("I", 1, 2),
    ("S2", 1, 0),
    ("S2", 0, 0),
    ("S1", 1, 2, 1),
    ("A", 2, 3),
    ("S1", 0, 2, 2),
    ("N", 1, 0),
    ("S1", 1, 2, 2),
    ("I", 1, 3),
    ("I", 1, 0),
    ("N", 0, 0),
    ("S2", 2, 0),
    ("Q1", 1, 0),
    ("S1", 2, 2, 1),
    ("S1", 2, 2, 2),
    ("Q1", 1, 1),
    ("S2", 0, 1),
    ("N", 2, 0),
    ("R", 0, 0),
    ("V", 0),
    ("B", 1, 0),
    ("S2", 2, 1),
    ("A", 2, 1),
    ("A", 2, 2),
    ("B", 0, 0),
    ("B", 2, 0),
    ("I", 2, 0),
    ("S2", 1, 1),
    ("I", 2, 1),
    ("N", 0, 1),
    ("N", 1, 1),
    ("N", 2, 1),
    ("I", 2, 2),
    ("B", 0, 1),
    ("T", 0, 0, 2),
    ("I", 2, 3),
    ("Q1", 2, 0),
    ("S2", 3, 1),
    ("B", 1, 1),
    ("K", 0, 0, 2),
    ("Q1", 2, 1),
    ("T", 1, 0, 2),
    ("S2", 3, 0),
    ("B", 2, 1),
    ("Q2", 0, 0, 2),
    ("S2", 0, 2),
    ("S2", 1, 2),
    ("R", 0, 1),
    ("N", 0, 2),
    ("S3", 0, 2, 0),
    ("N", 1, 2),
    ("S3", 0, 0, 0),
    ("N", 3, 0),
    ("R", 1, 1),
    ("K", 1, 0, 2),
    ("S2", 2, 2),
    ("B", 0, 2),
    ("R", 0, 2),
    ("S2", 3, 2),
    ("N", 3, 1),
    ("S3", 0, 2, 1),
    ("V", 1),
    ("S3", 0, 0, 1),
    ("B", 1, 2),
    ("T", 0, 2, 3),
    ("T", 2, 0, 2),
    ("T", 1, 2, 3),
    ("Q2", 1, 0, 2),
    ("K", 0, 2, 3),
    ("K", 2, 0, 2),
    ("S3", 0, 1, 0),
    ("Q2", 0, 2, 3),
    ("K", 1, 2, 3),
    ("S3", 1, 2, 0),
    ("S3", 1, 2, 1),
    ("S3", 0, 2, 2),
    ("N", 3, 2),
    ("N", 2, 2),
    ("B", 3, 2),
    ("S3", 0, 1, 1),
    ("X", 0, 2),
    ("S3", 1, 1, 0),
    ("S3", 1, 0, 0),
    ("R", 1, 0),
    ("Q2", 1, 2, 3),
    ("S3", 1, 0, 1),
    ("S3", 0, 1, 2),
    ("X", 0, 1),
    ("B", 3, 1),
    ("B", 3, 0),
    ("S3", 1, 1, 1),
    ("S3", 0, 0, 2),
    ("B", 2, 2),
    ("S3", 1, 0, 2),
    ("T", 3, 0, 2),
    ("Q2", 2, 0, 2),
    ("T", 3, 2, 3),
    ("T", 2, 2, 3),
    ("R", 2, 0),
    ("K", 3, 0, 2),
    ("K", 2, 2, 3),
    ("X", 0, 0),
    ("X", 1, 0),
    ("Q2", 3, 0, 2),
    ("S3", 2, 1, 0),
    ("S3", 2, 0, 0),
    ("S3", 2, 0, 1),
    ("S3", 2, 1, 1),
    ("Q2", 2, 2, 3),
    ("S3", 1, 1, 2),
    ("S3", 3, 1, 0),
    ("S3", 3, 0, 0),
    ("K", 3, 2, 3),
    ("S3", 2, 1, 2),
    ("S3", 3, 0, 1),
    ("Q2", 3, 2, 3),
    ("X", 1, 1),
    ("S3", 2, 0, 2),
    ("S3", 3, 0, 2),
    ("R", 2, 1),
    ("R", 3, 0),
    ("X", 2, 1),
    ("S3", 3, 2, 0),
    ("R", 3, 1),
    ("X", 2, 0),
    ("S3", 3, 1, 1),
    ("X", 3, 0),
    ("S3", 3, 1, 2),
    ("S3", 1, 2, 2),
    ("F", 2),
    ("F", 3),
    ("R", 1, 2),
    ("F", 0),
    ("F", 1),
    ("O", 2),
    ("X", 3, 1),
    ("O", 3),
    ("F", 4),
    ("F", 7),
    ("F", 5),
    ("O", 0),
    ("S3", 3, 2, 1),
    ("S3", 3, 2, 2),
    ("S3", 2, 2, 0),
    ("R", 3, 2),
    ("O", 4),
    ("O", 1),
    ("S3", 2, 2, 1),
    ("R", 2, 2),
    ("O", 7),
    ("S3", 2, 2, 2),
    ("X", 1, 2),
    ("X", 3, 2),
    ("O", 5),
    ("X", 2, 2),
    ("F", 6),
    ("O", 6),
    ("F", 8),
    ("F", 11),
    ("O", 8),
    ("F", 10),
    ("O", 11),
    ("F", 9),
    ("O", 9),
    ("O", 10),
]


def tile_plate_component_transfer_t2_kernel(
    tc, c, f_words, f_scales, d_words, d_scales, b_words, b_scales, v, r, out
):
    nc = tc.nc
    with ExitStack() as ctx:
        keep = ctx.enter_context(tc.tile_pool(name="keep", bufs=1))
        inter = ctx.enter_context(tc.tile_pool(name="inter", bufs=3))
        relay = ctx.enter_context(tc.tile_pool(name="relay", bufs=3))
        outp = ctx.enter_context(tc.tile_pool(name="outp", bufs=8))
        psum = ctx.enter_context(tc.psum_pool(name="psum", bufs=8))
        ctx.enter_context(tc.manual_schedule())

        def bank(shape, name, dtype=F32):
            return psum.tile(shape, dtype, name=name, tag="bank")

        warm = keep.tile([PART, 8], F32, name="warm")
        f_sc = keep.tile([PART, G * P], U8, name="f_sc", align_bytes=64)
        b_sc = keep.tile([PART, G * P], U8, name="b_sc", align_bytes=64)
        d_sc0 = keep.tile([PART, Q], U8, name="d_sc0", align_bytes=64)
        d_sc = keep.tile([PART, NT, PART], U8, name="d_sc", align_bytes=64)
        f_sb = keep.tile([PART, G, 2 * P], U8, name="f_sb", align_bytes=64)
        b_sb = keep.tile([PART, G, 2 * P], U8, name="b_sb", align_bytes=64)
        d_sb0 = keep.tile([PART, 2 * Q], U8, name="d_sb0", align_bytes=64)
        d_sb = keep.tile([PART, NT, 2 * PART], U8, name="d_sb", align_bytes=64)
        v_rows = keep.tile([PART, PART], BF16, name="v_rows", align_bytes=64)
        v_col = keep.tile([PART, P // PART], F32, name="v_col")
        r_bf = keep.tile([PART, NT], BF16, name="r_bf")
        r_col = keep.tile([PART, NT], F32, name="r_col")
        r_neg = keep.tile([PART, NT], F32, name="r_neg")
        ident = keep.tile([PART, PART], F32, name="ident", align_bytes=64)
        ident_b = keep.tile([PART, PART], BF16, name="ident_b", align_bytes=64)
        c_raw = []
        for g in range(G):
            c_g = keep.tile([PART, 4, Q], BF16, name="c_raw%d" % g, align_bytes=64)
            c_raw.append(c_g)

        nc.vector.memset(warm[:], 0.0)
        nc.scalar.activation(out=warm[:], in_=warm[:], func=COPY, scale=1.0)
        nc.vector.memset(f_sc[:].bitcast(I32), 0)
        nc.vector.memset(d_sc0[:].bitcast(I32), 0)
        make_identity(nc, ident[:])
        nc.gpsimd.memset(b_sc[:].bitcast(I32), 0)
        nc.gpsimd.memset(v_rows[:], 0.0)
        make_identity(nc, ident_b[:])

        def load_c(g):
            nc.sync.dma_start(
                out=c_raw[g][:], in_=c[g * 512 : (g + 1) * 512, :].rearrange("(p s) q -> p s q", s=4)
            )

        def load_f(jb):
            cols = slice(jb * 2 * JB, (jb + 1) * 2 * JB)
            nc.sync.dma_start(out=f_sb[:, :, cols], in_=f_words[:, :, cols].rearrange("g p n -> p g n"))

        def load_scales(queue, plane, scales, groups):
            dst = plane[:].bitcast(I32).rearrange("p (g n) -> p g n", g=groups)
            src = scales.bitcast(I32).rearrange("g (a b) n -> b a g n", b=4)
            for row in range(4):
                queue.dma_start(out=dst[row:PART:32, :, :], in_=src[row])

        load_c(0)
        load_scales(nc.sync, f_sc, f_scales, G)
        load_c(1)
        load_f(0)
        nc.sync.dma_start(out=d_sb0[:], in_=d_words[0])
        load_c(2)
        load_f(1)
        load_f(2)
        load_scales(nc.sync, d_sc0, d_scales, 1)
        nc.sync.dma_start(out=v_rows[0 : P // PART, :], in_=v.rearrange("(a b) -> a b", b=PART))
        nc.sync.dma_start(out=r_bf[:], in_=r.rearrange("(m t) -> m t", t=NT))
        load_scales(nc.sync, b_sc, b_scales, G)
        for g in range(G):
            nc.sync.dma_start(out=b_sb[:, g, :], in_=b_words[g])


        c_codes, c_sc, c1_codes, c1_sc = [], [], [], []
        for g in range(G):
            a0 = keep.tile([PART, Q], U32, name="c_codes%d" % g, align_bytes=64)
            a1 = keep.tile([PART, Q], U8, name="c_sc%d" % g, align_bytes=64)
            a2 = keep.tile([PART, JB], U32, name="c1_codes%d" % g, align_bytes=64)
            a3 = keep.tile([PART, JB], U8, name="c1_sc%d" % g, align_bytes=64)
            c_codes.append(a0)
            c_sc.append(a1)
            c1_codes.append(a2)
            c1_sc.append(a3)
        c2_codes, c2_sc, c2_t = [], [], []
        for t in range(NT):
            a0 = keep.tile([PART, G, PART], U32, name="c2_codes%d" % t, align_bytes=64)
            a1 = keep.tile([PART, G, PART], U8, name="c2_sc%d" % t, align_bytes=64)
            a2 = keep.tile([PART, G, PART, 4], BF16, name="c2_t%d" % t, align_bytes=64)
            c2_codes.append(a0)
            c2_sc.append(a1)
            c2_t.append(a2)
        c_t = keep.tile([PART, 2, P], F32, name="c_t", align_bytes=64)
        c1 = keep.tile([PART, NT, P], F32, name="c1", align_bytes=64)
        n2 = keep.tile([PART, NT, P], F32, name="n2", align_bytes=64)
        c2r = keep.tile([PART, NT, P], F32, name="c2r", align_bytes=64)
        c2b = keep.tile([PART, NT, G, 2, 256], BF16, name="c2b", align_bytes=64)
        x = keep.tile([PART, NT, P], F32, name="x", align_bytes=64)

        c_il = {}

        def interleave_c(g, part):
            if g not in c_il:
                c_il[g] = inter.tile([PART, NT, PART, 4], BF16, name="c_il%d" % g, tag="il", align_bytes=64)
            dst = c_il[g][:].rearrange("p t m s -> p m s t")
            src = c_raw[g][:].rearrange("p s (m t) -> p m s t", t=NT)
            if part == 0:
                nc.vector.tensor_copy(out=dst[:, 0:IL_SPLIT], in_=src[:, 0:IL_SPLIT])
            else:
                nc.scalar.copy(out=dst[:, IL_SPLIT:PART], in_=src[:, IL_SPLIT:PART])

        def quantize_c(g):
            nc.vector.quantize_mx(
                out=c_codes[g][:].bitcast(FP8X4),
                scales=c_sc[g][:],
                in_=c_il[g][:].rearrange("p t m s -> p (t m s)"),
            )

        ct = {}

        def turn_c(g):
            words = c_raw[g][:].rearrange("p s q -> p (s q)").bitcast(F32)
            for u in range(2):
                b = bank([PART, 4, PART], "ct%d%d" % (g, u))
                ct[(g, u)] = b
                for s in range(4):
                    nc.tensor.transpose(b[:, s, :], words[:, 256 * s + u : 256 * (s + 1) : 2], ident[:])

        def keep_c_t(g, u):
            nc.scalar.copy(
                out=c_t[:, u, g * 512 : (g + 1) * 512].rearrange("m (p s) -> m p s", s=4),
                in_=ct[(g, u)][:].rearrange("m s p -> m p s"),
            )

        acc = {}

        def stage1(g, jb, t):
            if g == 0:
                acc[(jb, t)] = bank([PART, JB], "acc%d%d" % (jb, t))
            nc.tensor.matmul_mx(
                out=acc[(jb, t)][:],
                lhsT=c_codes[g][:, t * PART : (t + 1) * PART].bitcast(FP8X4),
                lhsT_scale=c_sc[g][:, t * PART : (t + 1) * PART],
                rhs=f_sb[:, g, jb * 2 * JB : (jb + 1) * 2 * JB].bitcast(FP4X4),
                rhs_scale=f_sc[:, g * P + jb * JB : g * P + (jb + 1) * JB],
                start=(g == 0),
                stop=(g == G - 1),
            )

        c_t_bf = c_t[:].rearrange("m u j -> m (u j)").bitcast(BF16).rearrange("m (u j e) -> m u j e", u=2, e=2)

        def add_c(jb, t):
            cols = slice(jb * JB, (jb + 1) * JB)
            if (jb, t) in RELAY_A:
                tmp = relay.tile([PART, JB], F32, name="ra%d%d" % (jb, t), tag="relay", align_bytes=64)
                nc.scalar.copy(out=tmp[:], in_=acc[(jb, t)][:])
                nc.gpsimd.tensor_tensor(out=c1[:, t, cols], in0=tmp[:], in1=c_t_bf[:, t // 2, cols, t % 2], op=ALU.add)
                return
            nc.vector.tensor_tensor(
                out=c1[:, t, cols], in0=acc[(jb, t)][:], in1=c_t_bf[:, t // 2, cols, t % 2], op=ALU.add
            )

        c1_il = {}

        def interleave_c1(jb, k):
            if jb not in c1_il:
                c1_il[jb] = inter.tile([PART, JB, NT], BF16, name="c1_il%d" % jb, tag="il", align_bytes=64)
            cols = slice(k * 128, (k + 1) * 128)
            dst = c1_il[jb][:, cols, :].rearrange("m (j i) t -> m j t i", i=4)
            src = c1[:, :, jb * JB + k * 128 : jb * JB + (k + 1) * 128].rearrange("m t (j i) -> m j t i", i=4)
            if I_ENGINE[jb][k] == "v":
                nc.vector.tensor_copy(out=dst, in_=src)
            elif I_ENGINE[jb][k] == "g":
                nc.gpsimd.tensor_scalar(out=dst, in0=src, scalar1=1.0, scalar2=0.0, op0=ALU.mult, op1=ALU.add)
            else:
                nc.scalar.copy(out=dst, in_=src)

        def quantize_c1(jb, h):
            cols = slice(h * 256, (h + 1) * 256)
            nc.vector.quantize_mx(
                out=c1_codes[jb][:, cols].bitcast(FP8X4),
                scales=c1_sc[jb][:, cols],
                in_=c1_il[jb][:, cols, :].rearrange("m j t -> m (j t)"),
            )

        push = {}

        def stage2(t, jb):
            b = bank([PART, JB], "push%d%d" % (t, jb))
            push[(t, jb)] = b
            nc.tensor.matmul_mx(
                out=b[:],
                lhsT=d_sb[:, t, :].bitcast(FP4X4),
                lhsT_scale=d_sc[:, t, :],
                rhs=c1_codes[jb][:].bitcast(FP8X4),
                rhs_scale=c1_sc[jb][:],
                start=True,
                stop=True,
            )

        def displace_n(t, jb):
            cols = slice(jb * JB, (jb + 1) * JB)
            nc.vector.scalar_tensor_tensor(
                out=n2[:, t, cols], in0=push[(t, jb)][:], scalar=0.0, in1=c1[:, t, cols], op0=ALU.max, op1=ALU.subtract
            )

        def displace_b(t, jb):
            cols = slice(jb * JB, (jb + 1) * JB)
            nc.scalar.activation(
                out=c2b[:, t, jb, :, :].rearrange("m u (w e) -> m u w e", e=2),
                in_=n2[:, t, cols].rearrange("m (w u e) -> m u w e", u=2, e=2),
                func=COPY,
                scale=-1.0,
            )

        def scale_c2(t, jb):
            cols = slice(jb * JB, (jb + 1) * JB)
            if R_ENGINE[t][jb] == "s":
                nc.scalar.activation(out=c2r[:, t, cols], in_=n2[:, t, cols], func=COPY, scale=r_neg[:, t : t + 1])
            elif R_ENGINE[t][jb] == "v":
                nc.vector.tensor_scalar(
                    out=c2r[:, t, cols], in0=n2[:, t, cols], scalar1=r_neg[:, t : t + 1], scalar2=None, op0=ALU.mult
                )
            else:
                nc.gpsimd.tensor_scalar(
                    out=c2r[:, t, cols], in0=n2[:, t, cols], scalar1=r_neg[:, t : t + 1], scalar2=0.0,
                    op0=ALU.mult, op1=ALU.add,
                )

        def turn_c2(t, j0, j1):
            n = j1 - j0
            b = bank([PART, n, 2, PART], "c2t%d%d" % (t, j0))
            for jb in range(j0, j1):
                for u in range(2):
                    nc.tensor.transpose(b[:, jb - j0, u, :], c2b[:, t, jb, u, :].bitcast(F32), ident[:])
            c2ps[(t, j0)] = b

        c2ps = {}

        def keep_c2(t, j0, j1):
            b = c2ps[(t, j0)]
            dst = c2_t[t][:].rearrange("p g m k -> p (g m k)").bitcast(F32).rearrange("p (g m u) -> p g m u", g=G, u=2)
            nc.scalar.copy(out=dst[:, j0:j1, :, :], in_=b[:].rearrange("p g u m -> p g m u"))

        def quantize_c2(t, j0, j1):
            nc.vector.quantize_mx(
                out=c2_codes[t][:, j0:j1, :].rearrange("p g m -> p (g m)").bitcast(FP8X4),
                scales=c2_sc[t][:, j0:j1, :].rearrange("p g m -> p (g m)"),
                in_=c2_t[t][:, j0:j1, :, :].rearrange("p g m k -> p (g m k)"),
            )

        back = {}

        def stage3(t, jb, g):
            if g == 0:
                back[(t, jb)] = bank([PART, JB], "back%d%d" % (t, jb))
            nc.tensor.matmul_mx(
                out=back[(t, jb)][:],
                lhsT=c2_codes[t][:, g, :].bitcast(FP8X4),
                lhsT_scale=c2_sc[t][:, g, :],
                rhs=b_sb[:, g, jb * 2 * JB : (jb + 1) * 2 * JB].bitcast(FP4X4),
                rhs_scale=b_sc[:, g * P + jb * JB : g * P + (jb + 1) * JB],
                start=(g == 0),
                stop=(g == G - 1),
            )

        def add_c2(t, jb):
            cols = slice(jb * JB, (jb + 1) * JB)
            if (t, jb) in RELAY_X:
                tmp = relay.tile([PART, JB], F32, name="rx%d%d" % (t, jb), tag="relay", align_bytes=64)
                nc.scalar.activation(out=tmp[:], in_=back[(t, jb)][:], func=COPY, scale=r_col[:, t : t + 1])
                nc.gpsimd.tensor_tensor(out=x[:, t, cols], in0=tmp[:], in1=c2r[:, t, cols], op=ALU.add)
                return
            nc.vector.scalar_tensor_tensor(
                out=x[:, t, cols], in0=back[(t, jb)][:], scalar=r_col[:, t : t + 1], in1=c2r[:, t, cols],
                op0=ALU.mult, op1=ALU.add,
            )

        fin = {}

        def turn_x(tile_no):
            b = bank([PART, NT, PART], "fin%d" % tile_no)
            fin[tile_no] = b
            for t in range(NT):
                nc.tensor.transpose(b[:, t, :], x[:, t, tile_no * PART : (tile_no + 1) * PART], ident[:])

        def store(tile_no):
            o = outp.tile([PART, PART, NT], F32, name="o%d" % tile_no, tag="o", align_bytes=64)
            src = fin[tile_no][:].rearrange("p t m -> p m t")
            scale = v_col[:, tile_no : tile_no + 1]
            if tile_no in O_SCALAR:
                nc.scalar.activation(out=o[:], in_=src, func=COPY, scale=scale)
            else:
                nc.vector.tensor_scalar(out=o[:], in0=src, scalar1=scale, scalar2=None, op0=ALU.mult)
            nc.sync.dma_start(
                out=out[tile_no * PART : (tile_no + 1) * PART, :], in_=o[:].rearrange("p m t -> p (m t)")
            )

        def permute_d(part):
            if part == 0:
                nc.vector.tensor_copy(
                    out=d_sb[:].rearrange("p t (m b) -> p t m b", b=2),
                    in_=d_sb0[:].rearrange("p (m t b) -> p t m b", t=NT, b=2),
                )
            elif part == 1:
                nc.vector.tensor_copy(out=d_sc[:], in_=d_sc0[:].rearrange("p (m t) -> p t m", t=NT))
            elif part == 2:
                nc.vector.tensor_copy(out=r_col[:], in_=r_bf[:])
            else:
                nc.vector.tensor_scalar(out=r_neg[:], in0=r_bf[:], scalar1=-1.0, scalar2=None, op0=ALU.mult)

        v_ps = {}

        def turn_v(part):
            if part == 0:
                v_ps[0] = bank([PART, PART], "v_ps", BF16)
                nc.tensor.transpose(v_ps[0][:], v_rows[:], ident_b[:])
            else:
                nc.scalar.copy(out=v_col[:], in_=v_ps[0][:, 0 : P // PART])

        steps = dict(
            CT=turn_c, KC=keep_c_t, IL=interleave_c, QC=quantize_c, S1=stage1, A=add_c,
            I=interleave_c1, Q1=quantize_c1, S2=stage2, N=displace_n, B=displace_b, R=scale_c2, T=turn_c2,
            K=keep_c2, Q2=quantize_c2, S3=stage3, X=add_c2, F=turn_x, O=store, D=permute_d, V=turn_v,
        )
        for step in ORDER:
            steps[step[0]](*step[1:])
